import numpy as np
import ml_dtypes


def mxq(x, axis, fmt="e4m3"):
    dtype, down = {"e4m3": (ml_dtypes.float8_e4m3fn, 7), "e5m2": (ml_dtypes.float8_e5m2, 14)}[fmt]
    v = np.moveaxis(np.asarray(x, np.float32).astype(ml_dtypes.bfloat16).astype(np.float64), axis, -1)
    blocks = v.reshape(v.shape[:-1] + (-1, 32))
    amax = np.abs(blocks).max(-1, keepdims=True)
    byte = np.maximum(np.where(amax > 0, np.frexp(amax)[1] - 1 + 127, 0) - down, 1)
    scale = np.exp2(byte - 127.0)
    codes = (blocks / scale).astype(np.float32).astype(dtype).astype(np.float64)
    return np.moveaxis((codes * scale).reshape(v.shape), -1, axis)


WIDE = False


def mx_kscale(k):
    if not WIDE:
        return np.ones(k)
    levels = np.array([10, -10, 5, -5, 0])
    if k % 512:
        return np.exp2(np.random.permutation(np.resize(levels, k // 32))).repeat(32)
    a = np.empty((k // 512, 16))
    for p in range(k // 512):
        a[p, :8] = np.random.permutation(np.resize(levels, 8))
        for g in range(8):
            far = levels[np.abs(levels - a[p, g]) >= 10]
            a[p, g + 8] = far[np.random.randint(len(far))]
    return np.exp2(a.ravel()).repeat(32)


def f64(x):
    return np.asarray(x).astype(np.float64)


def striped(idx):
    return np.tile(idx.reshape(-1, 16).T, (8, 1)).astype(np.uint16)


def unstriped(offs):
    return offs[:16].T.reshape(-1).astype(np.int64)


def striped8(idx):
    return np.concatenate([x.reshape(-1, 16).T for x in idx]).astype(np.uint16)


def runs(offs, k):
    lists = np.stack([offs[16 * r : 16 * r + 16].T.reshape(-1) for r in range(8)]).astype(np.int64)
    return lists[np.arange(k) % 512 // 64]


def pack_weight(w):
    k, n = w.shape
    w = f64(np.asarray(w, np.float32).astype(ml_dtypes.bfloat16)).reshape(k // 32, 32, n)
    amax = np.abs(w).max(1)
    byte = np.clip(np.where(amax > 0, np.frexp(amax)[1] - 1 + 127 - 7, 1), 1, 254)
    scaled = (w * np.exp2(127.0 - byte)[:, None, :]).reshape(k, n).astype(np.float32)
    words = np.ascontiguousarray(scaled.reshape(k // 512, 128, 4, n).transpose(0, 1, 3, 2)).astype(ml_dtypes.float8_e4m3fn).view(np.uint8)
    return words, np.ascontiguousarray(byte.astype(np.uint8).reshape(k // 512, 16, n))


def unpack_weight(words, scales):
    g, p, n, _ = words.shape
    vals = np.ascontiguousarray(words).view(ml_dtypes.float8_e4m3fn).astype(np.float64) * np.repeat(np.exp2(scales.astype(np.float64) - 127.0), 8, axis=1)[..., None]
    return vals.transpose(0, 1, 3, 2).reshape(g * 512, n)


K, T, S, N, H, G, W = 512, 1024, 512, 512, 512, 2048, 1024


def setup_inputs():
    n = np.random.standard_normal
    s = mx_kscale(K)[:, None]
    u = mx_kscale(S)
    packed_xT = pack_weight(n((K, T)) * s)
    packed_dT = pack_weight(n((K, G)) / s)
    return {
        "x_words": packed_xT[0],
        "x_scales": packed_xT[1],
        "w1": (n((K, H)) / np.sqrt(K) / s).astype(np.float32),
        "d_words": packed_dT[0],
        "d_scales": packed_dT[1],
        "gn": (np.random.uniform(0.5, 1.5, (H, 1)) * u[:, None]).astype(np.float32),
        "gk": (np.random.uniform(0.5, 1.5, (H, 1)) * u[:, None]).astype(np.float32),
        "w2": (n((H, N)) / np.sqrt(2 * H) / u[:, None]).astype(np.float32),
        "w3": (n((H, N)) / np.sqrt(2 * H) / u[:, None]).astype(np.float32),
        "offs": striped(np.random.permutation(T)[:S]),
        "kidx": striped8(np.random.randint(0, G, (8, H))),
        "two": striped(np.random.permutation(T)[:S]),
        "n1": striped(np.random.randint(0, S, W)),
        "n2": striped(np.random.permutation(S)),
        "n3": striped(np.random.permutation(S)),
        "n4": striped(np.random.permutation(S)),
        "n5": striped(np.random.randint(0, S, G)),
    }


def reference(x_words, x_scales, w1, d_words, d_scales, gn, gk, w2, w3, offs, kidx, two, n1, n2, n3, n4, n5):
    xq = unpack_weight(x_words, x_scales)[:, unstriped(offs)]
    y = mxq(f64(w1), 0, "e4m3").T @ xq
    mb = y[:, unstriped(n1)]
    mx = mb.reshape(H, S, 2).max(axis=2)
    st = y - mx
    z = f64(gn) * (np.maximum(st, st[:, unstriped(n2)]))
    d_kidx = unpack_weight(d_words, d_scales)[np.arange(K)[:, None], runs(kidx, K)]
    x_two = unpack_weight(x_words, x_scales)[:, unstriped(two)]
    s = 0.0625 * (d_kidx.T @ x_two)
    st2 = s - s[:, unstriped(n3)]
    z2 = f64(gk) * (st2 / (np.abs(st2[:, unstriped(n4)]) + 0.5))
    h = mxq(f64(w2), 0, "e4m3").T @ mxq(z, 0, "e4m3") + mxq(f64(w3), 0, "e4m3").T @ mxq(z2, 0, "e4m3")
    ex = np.exp(h)
    mb2 = ex[:, unstriped(n5)]
    ms = mb2.reshape(N, S, 4).sum(axis=2)
    return np.log(ms + ex) - h

@@ -1,0 +1,255 @@
+from contextlib import ExitStack
+
+import concourse.mybir as mybir
+
+K, T, S, N, H, G = 512, 1024, 512, 512, 512, 2048
+FLOPS = 4 * 2 * 512 * 512 * 512
+
+F32 = mybir.dt.float32
+BF16 = mybir.dt.bfloat16
+I32 = mybir.dt.int32
+U32 = mybir.dt.uint32
+U16 = mybir.dt.uint16
+U8 = mybir.dt.uint8
+FP8X4 = mybir.dt.float8_e4m3fn_x4
+ALU = mybir.AluOpType
+ACT = mybir.ActivationFunctionType
+
+P = 128
+PACK = 4
+LIST_ROWS = 16
+HALF = S // 2
+
+
+def tile_picked_jkeyghopmhopnglse_none_p_kernel(tc, x_words, x_scales, w1, d_words, d_scales, gn, gk, w2, w3, offs, kidx, two, n1, n2, n3, n4, n5, out):
+    nc = tc.nc
+
+    with ExitStack() as ctx:
+        lists = ctx.enter_context(tc.tile_pool(name="lists", bufs=1))
+        keep = ctx.enter_context(tc.tile_pool(name="keep", bufs=1))
+        ring = ctx.enter_context(tc.tile_pool(name="ring", bufs=3))
+        psum = ctx.enter_context(tc.psum_pool(name="psum", bufs=1))
+
+        def load_list(src, name):
+            tile = lists.tile(list(src.shape), U16, name=name)
+            nc.sync.dma_start(tile[:], src)
+            return tile
+
+        def entries(tile, first, count):
+            return tile[:, first // LIST_ROWS : (first + count) // LIST_ROWS]
+
+        def by_lines(ap):
+            return ap.rearrange("p (t c i) -> p c t i", t=PACK, i=PACK)
+
+        def woven(ap):
+            return ap.rearrange("p (c i t) -> p c t i", t=PACK, i=PACK)
+
+        def quantize(values, name):
+            width = values.shape[1] // PACK
+            codes = keep.tile([P, width], U32, align_bytes=64, name=name + "_codes")
+            scales = keep.tile([P, width], U8, align_bytes=64, name=name + "_scales")
+            nc.vector.quantize_mx(out=codes[:].bitcast(FP8X4), scales=scales[:], in_=values)
+            return codes, scales
+
+        def product(acc, left, cols, right, start, stop):
+            nc.tensor.matmul_mx(
+                out=acc,
+                lhsT=left[0][:, cols].bitcast(FP8X4),
+                lhsT_scale=left[1][:, cols],
+                rhs=right[0][:].bitcast(FP8X4),
+                rhs_scale=right[1][:],
+                start=start,
+                stop=stop,
+            )
+
+        x_bytes = keep.tile([P, T], U8, name="x_bytes")
+        d_bytes = keep.tile([P, G], U8, name="d_bytes")
+        key_scales = keep.tile([P, H], U8, align_bytes=64, name="key_scales")
+        for tile in (x_bytes, d_bytes, key_scales):
+            nc.vector.memset(tile[:].bitcast(I32), 0)
+
+        offs_sb = load_list(offs, "offs_sb")
+        x_table = keep.tile([P, T], U32, name="x_table")
+        nc.sync.dma_start(x_table[:].bitcast(I32), x_words[0].rearrange("p n t -> p (n t)").bitcast(I32))
+        for q in range(4):
+            nc.sync.dma_start(x_bytes[32 * q : 32 * q + 4, :].bitcast(I32), x_scales[0, 4 * q : 4 * q + 4, :].bitcast(I32))
+        w1_raw = []
+        for u in range(2):
+            raw = keep.tile([P, PACK, HALF], F32, name="w1_raw%d" % u)
+            nc.sync.dma_start(raw[:], w1[:, u * HALF : (u + 1) * HALF].rearrange("(p j) c -> p j c", j=PACK))
+            w1_raw.append(raw)
+        gn_sb = keep.tile([P, PACK], F32, name="gn_sb")
+        nc.sync.dma_start(gn_sb[:], gn.rearrange("(p t) o -> p (t o)", t=PACK))
+        n1_sb = load_list(n1, "n1_sb")
+        kidx_sb = load_list(kidx, "kidx_sb")
+        for r in range(2):
+            nc.sync.dma_start(d_bytes[r:P:LIST_ROWS, :].bitcast(I32), d_scales[0, r:16:2, :].bitcast(I32))
+        two_sb = load_list(two, "two_sb")
+        d_table = keep.tile([P, G], U32, name="d_table")
+        nc.sync.dma_start(d_table[:].bitcast(I32), d_words[0].rearrange("p n t -> p (n t)").bitcast(I32))
+        gk_sb = keep.tile([P, PACK], F32, name="gk_sb")
+        nc.sync.dma_start(gk_sb[:], gk.rearrange("(p t) o -> p (t o)", t=PACK))
+        n3_sb = load_list(n3, "n3_sb")
+        n4_sb = load_list(n4, "n4_sb")
+        n2_sb = load_list(n2, "n2_sb")
+        n5_sb = load_list(n5, "n5_sb")
+
+        def gather_codes(table, table_bytes, offsets, name):
+            words = keep.tile([P, S], U32, align_bytes=64, name=name + "_words", tag=name + "_words")
+            scales = keep.tile([P, S], U8, align_bytes=64, name=name + "_bytes")
+            nc.vector.tensor_copy(words[:], table[:].indirect(offsets[:]))
+            nc.vector.tensor_copy(scales[:], table_bytes[:].indirect(offsets[:]))
+            return words, scales
+
+        x_idx = gather_codes(x_table, x_bytes, offs_sb, "x_idx")
+        w1_bf = keep.tile([P, PACK * H], BF16, align_bytes=64, name="w1_bf")
+        w1_dealt = w1_bf[:].rearrange("p (t m j) -> p m j t", t=PACK, j=PACK)
+        for u in range(2):
+            nc.scalar.copy(w1_dealt[:, u * (P // 2) : (u + 1) * (P // 2)], w1_raw[u][:].rearrange("p j (m t) -> p m j t", t=PACK))
+        w1_q = quantize(w1_bf[:], "w1")
+
+        gn_neg = keep.tile([P, PACK], F32, name="gn_neg")
+        gn_sign = keep.tile([P, PACK], F32, name="gn_sign")
+        gn_abs = keep.tile([P, PACK], F32, name="gn_abs")
+        nc.gpsimd.tensor_scalar(gn_neg[:], gn_sb[:], 0.0, -2.0, ALU.is_lt, ALU.mult)
+        nc.gpsimd.tensor_scalar(gn_sign[:], gn_neg[:], 1.0, 1.0, ALU.mult, ALU.add)
+        nc.gpsimd.tensor_tensor(gn_abs[:], gn_sb[:], gn_sign[:], ALU.mult)
+
+        banks_a = [psum.tile([P, S], F32, name="y_acc%d" % t, tag="bank_a%d" % t) for t in range(PACK)]
+        for t in range(PACK):
+            product(banks_a[t][:], w1_q, slice(t * P, (t + 1) * P), x_idx, True, True)
+
+        key_bytes = keep.tile([P, H], U8, name="key_bytes")
+        nc.vector.tensor_copy(key_bytes[:], d_bytes[:].indirect(kidx_sb[:]))
+        key_bytes_dealt = keep.tile([P, H], U8, name="key_bytes_dealt", tag="dealt_w_raw")
+        nc.vector.tensor_copy(key_bytes_dealt[:].rearrange("p (t m) -> p m t", t=PACK), key_bytes[:].rearrange("p (m t) -> p m t", t=PACK))
+        for odd in range(2):
+            for r in range(2):
+                nc.sync.dma_start(
+                    key_scales[2 * odd + r : P : 32, :].bitcast(I32),
+                    key_bytes_dealt[LIST_ROWS * odd + r : P : 32, :].bitcast(I32),
+                )
+        w_raw = keep.tile([P, 2 * PACK * N], F32, name="w_raw", tag="dealt_w_raw")
+        w3_raw, w2_raw = w_raw[:, : PACK * N], w_raw[:, PACK * N :]
+        nc.sync.dma_start(w3_raw, w3.rearrange("(p j) c -> p (j c)", j=PACK))
+        nc.sync.dma_start(w2_raw, w2.rearrange("(p j) c -> p (j c)", j=PACK))
+        x_two = gather_codes(x_table, x_bytes, two_sb, "x_two")
+        key_words = keep.tile([P, H], U32, name="key_words")
+        nc.vector.tensor_copy(key_words[:], d_table[:].indirect(kidx_sb[:]))
+        key_codes = keep.tile([P, H], U32, align_bytes=64, name="key_codes", tag="key_codes")
+        nc.vector.tensor_copy(key_codes[:].rearrange("p (t m) -> p m t", t=PACK), key_words[:].rearrange("p (m t) -> p m t", t=PACK))
+        banks_b = [psum.tile([P, S], F32, name="s_acc%d" % t, tag="bank_b%d" % t) for t in range(PACK)]
+        for t in range(PACK):
+            product(banks_b[t][:], (key_codes, key_scales), slice(t * P, (t + 1) * P), x_two, True, True)
+
+        gk_zero = keep.tile([P, PACK], F32, name="gk_zero")
+        gk_safe = keep.tile([P, PACK], F32, name="gk_safe")
+        gk_rec = keep.tile([P, PACK], F32, name="gk_rec")
+        gk_inv = keep.tile([P, PACK], F32, name="gk_inv")
+        nc.gpsimd.tensor_scalar(gk_zero[:], gk_sb[:], 0.0, 1.0, ALU.is_equal, ALU.mult)
+        nc.gpsimd.tensor_tensor(gk_safe[:], gk_sb[:], gk_zero[:], ALU.add)
+        nc.vector.reciprocal(gk_rec[:], gk_safe[:])
+        nc.vector.scalar_tensor_tensor(gk_inv[:], gk_rec[:], -1.0, gk_rec[:], ALU.mult, ALU.max)
+
+        wide = [keep.tile([P, PACK * S], F32, name="wide%d" % t) for t in range(PACK)]
+        y = []
+        for t in range(PACK):
+            tile = keep.tile([P, S], F32, name="y%d" % t)
+            nc.scalar.activation(tile[:], banks_a[t][:], ACT.Copy, scale=gn_abs[:, t : t + 1])
+            for first, count in ((0, 352), (352, 352), (704, 320)):
+                nc.scalar.activation(wide[t][:, S + first : S + first + count], tile[:].indirect(entries(n1_sb, first, count)), ACT.Copy)
+            y.append(tile)
+
+        num = keep.tile([P, PACK * S], F32, name="num")
+        size = keep.tile([P, PACK * S], F32, name="size", tag="size_recip")
+        s = keep.tile([P, PACK * S], F32, name="s", tag="s_mx")
+        plane = [slice(t * S, (t + 1) * S) for t in range(PACK)]
+        for t in range(PACK):
+            nc.vector.tensor_scalar(s[:, plane[t]], banks_b[t][:], gk_sb[:, t : t + 1], 0.0625, ALU.mult, ALU.mult)
+        for step in range(PACK + 1):
+            if step < PACK:
+                for u in range(2):
+                    nc.vector.tensor_copy(
+                        wide[step][:, 3 * S + u * HALF : 3 * S + (u + 1) * HALF], s[:, plane[step]].indirect(entries(n3_sb, u * HALF, HALF))
+                    )
+            if step >= 1:
+                t = step - 1
+                nc.vector.tensor_tensor(num[:, plane[t]], s[:, plane[t]], wide[t][:, 3 * S :], ALU.subtract)
+                nc.scalar.activation(size[:, plane[t]], num[:, plane[t]], ACT.Abs)
+                nc.scalar.activation(wide[t][:, :S], size[:, plane[t]], ACT.Ln, bias=0.5, scale=gk_inv[:, t : t + 1])
+        recip = keep.tile([P, PACK * S], F32, name="recip", tag="size_recip")
+        for t in range(PACK):
+            nc.scalar.activation(recip[:, t * S : (t + 1) * S], wide[t][:].indirect(n4_sb[:]), ACT.Exp, scale=-1.0)
+
+        st = keep.tile([P, PACK * S], F32, name="st")
+        mx = keep.tile([P, PACK * S], F32, name="mx", tag="s_mx")
+        for t in range(PACK):
+            nc.vector.tensor_tensor(mx[:, plane[t]], wide[t][:, S : 3 * S : 2], wide[t][:, S + 1 : 3 * S : 2], ALU.max)
+        for t in range(PACK):
+            nc.vector.tensor_tensor(st[:, t * S : (t + 1) * S], y[t][:], mx[:, plane[t]], ALU.subtract)
+
+        w3_bf = keep.tile([P, PACK * N], BF16, align_bytes=64, name="w3_bf", tag="key_codes")
+        nc.vector.tensor_copy(woven(w3_bf[:]), by_lines(w3_raw))
+        w2_bf = keep.tile([P, PACK * N], BF16, align_bytes=64, name="w2_bf", tag="x_two_words")
+        nc.vector.tensor_tensor(
+            woven(w2_bf[:]), by_lines(w2_raw), gn_sign[:].unsqueeze(1).unsqueeze(3).to_broadcast([P, N // PACK, PACK, PACK]), ALU.mult
+        )
+        w3_q = quantize(w3_bf[:], "w3")
+        w2_q = quantize(w2_bf[:], "w2")
+
+        z2_bf = keep.tile([P, PACK * S], BF16, align_bytes=64, name="z2_bf")
+        nc.vector.tensor_tensor(woven(z2_bf[:]), by_lines(num[:]), by_lines(recip[:]), ALU.mult)
+        z2_q = quantize(z2_bf[:], "z2")
+        h = [psum.tile([P, S], F32, name="h_acc%d" % t, tag="bank_a%d" % t) for t in range(N // P)]
+        for t in range(N // P):
+            product(h[t][:], w3_q, slice(t * P, (t + 1) * P), z2_q, True, False)
+
+        for first, count in ((0, 256), (256, 128), (384, 128)):
+            other = keep.tile([P, PACK * count], F32, name="other%d" % first)
+            for t in range(PACK):
+                nc.scalar.activation(other[:, t * count : (t + 1) * count], st[:, plane[t]].indirect(entries(n2_sb, first, count)), ACT.Copy)
+            z_bf = keep.tile([P, PACK * count], BF16, align_bytes=64, name="z_bf%d" % first)
+            nc.vector.tensor_tensor(woven(z_bf[:]), by_lines(st[:])[:, first // PACK : (first + count) // PACK], by_lines(other[:]), ALU.max)
+            z_q = quantize(z_bf[:], "z%d" % first)
+            for t in range(N // P):
+                product(h[t][:, first : first + count], w2_q, slice(t * P, (t + 1) * P), z_q, False, first + count == S)
+
+        for t in range(N // P):
+            nc.scalar.activation(wide[t][:, :S], h[t][:], ACT.Exp)
+
+        units = [(0, 0, S), (1, 0, S), (2, 0, S), (3, 0, HALF), (3, HALF, HALF)]
+        members = {}
+        totals = {}
+
+        def fetch(t, first, count):
+            tile = ring.tile([P, 4 * count], F32, name="members")
+            cut = 4 * count * 3 // 8
+            nc.vector.tensor_copy(tile[:, :cut], wide[t][:].indirect(entries(n5_sb, 4 * first, cut)))
+            nc.scalar.activation(tile[:, cut:], wide[t][:].indirect(entries(n5_sb, 4 * first + cut, 4 * count - cut)), ACT.Copy)
+            members[t, first] = tile
+
+        def add_up(t, first, count):
+            quads = members[t, first][:].rearrange("p (j e) -> p j e", e=4)
+            pairs = ring.tile([P, count, 2], F32, name="pairs", bufs=2)
+            nc.vector.tensor_tensor(pairs[:], quads[:, :, 0:2], quads[:, :, 2:4], ALU.add)
+            part = ring.tile([P, count], F32, name="part", bufs=2)
+            nc.vector.tensor_tensor(part[:], pairs[:, :, 0], wide[t][:, first : first + count], ALU.add)
+            total = ring.tile([P, count], F32, name="total", bufs=2)
+            nc.vector.tensor_tensor(total[:], pairs[:, :, 1], part[:], ALU.add)
+            totals[t, first] = total
+
+        def finish(t, first, count):
+            cols = slice(first, first + count)
+            logs = ring.tile([P, count], F32, name="logs", bufs=2)
+            nc.scalar.activation(logs[:], totals[t, first][:], ACT.Ln)
+            result = ring.tile([P, count], F32, name="result", bufs=2)
+            nc.vector.tensor_tensor(result[:], logs[:], h[t][:, cols], ALU.subtract)
+            nc.sync.dma_start(out[t * P : (t + 1) * P, cols], result[:])
+
+        for step in range(len(units) + 2):
+            if step < len(units):
+                fetch(*units[step])
+            if 1 <= step <= len(units):
+                add_up(*units[step - 1])
+            if step >= 2:
+                finish(*units[step - 2])

@@ -27,7 +27,6 @@ def tile_picked_jkeyghopmhopnglse_none_p_kernel(tc, x_words, x_scales, w1, d_wor
     with ExitStack() as ctx:
         lists = ctx.enter_context(tc.tile_pool(name="lists", bufs=1))
         keep = ctx.enter_context(tc.tile_pool(name="keep", bufs=1))
-        ring = ctx.enter_context(tc.tile_pool(name="ring", bufs=3))
         psum = ctx.enter_context(tc.psum_pool(name="psum", bufs=1))
 
         def load_list(src, name):
@@ -75,34 +74,28 @@ def tile_picked_jkeyghopmhopnglse_none_p_kernel(tc, x_words, x_scales, w1, d_wor
             nc.sync.dma_start(x_bytes[32 * q : 32 * q + 4, :].bitcast(I32), x_scales[0, 4 * q : 4 * q + 4, :].bitcast(I32))
         w1_raw = []
         for u in range(2):
-            raw = keep.tile([P, PACK, HALF], F32, name="w1_raw%d" % u)
+            raw = keep.tile([P, PACK, HALF], F32, name="w1_raw%d" % u, tag=("w1_raw", "dealt_w_raw")[u])
             nc.sync.dma_start(raw[:], w1[:, u * HALF : (u + 1) * HALF].rearrange("(p j) c -> p j c", j=PACK))
             w1_raw.append(raw)
-        gn_sb = keep.tile([P, PACK], F32, name="gn_sb")
-        nc.sync.dma_start(gn_sb[:], gn.rearrange("(p t) o -> p (t o)", t=PACK))
-        n1_sb = load_list(n1, "n1_sb")
         kidx_sb = load_list(kidx, "kidx_sb")
         for r in range(2):
             nc.sync.dma_start(d_bytes[r:P:LIST_ROWS, :].bitcast(I32), d_scales[0, r:16:2, :].bitcast(I32))
         two_sb = load_list(two, "two_sb")
+        gn_sb = keep.tile([P, PACK], F32, name="gn_sb")
+        nc.sync.dma_start(gn_sb[:], gn.rearrange("(p t) o -> p (t o)", t=PACK))
+        n1_sb = load_list(n1, "n1_sb")
         d_table = keep.tile([P, G], U32, name="d_table")
         nc.sync.dma_start(d_table[:].bitcast(I32), d_words[0].rearrange("p n t -> p (n t)").bitcast(I32))
-        gk_sb = keep.tile([P, PACK], F32, name="gk_sb")
-        nc.sync.dma_start(gk_sb[:], gk.rearrange("(p t) o -> p (t o)", t=PACK))
-        n3_sb = load_list(n3, "n3_sb")
-        n4_sb = load_list(n4, "n4_sb")
-        n2_sb = load_list(n2, "n2_sb")
-        n5_sb = load_list(n5, "n5_sb")
 
-        def gather_codes(table, table_bytes, offsets, name):
-            words = keep.tile([P, S], U32, align_bytes=64, name=name + "_words", tag=name + "_words")
-            scales = keep.tile([P, S], U8, align_bytes=64, name=name + "_bytes")
+        def gather_codes(table, table_bytes, offsets, name, words_tag):
+            words = keep.tile([P, S], U32, align_bytes=64, name=name + "_words", tag=words_tag)
+            scales = keep.tile([P, S], U8, align_bytes=64, name=name + "_bytes", tag="token_bytes")
             nc.vector.tensor_copy(words[:], table[:].indirect(offsets[:]))
             nc.vector.tensor_copy(scales[:], table_bytes[:].indirect(offsets[:]))
             return words, scales
 
-        x_idx = gather_codes(x_table, x_bytes, offs_sb, "x_idx")
-        w1_bf = keep.tile([P, PACK * H], BF16, align_bytes=64, name="w1_bf")
+        x_idx = gather_codes(x_table, x_bytes, offs_sb, "x_idx", "x_idx_words")
+        w1_bf = keep.tile([P, PACK * H], BF16, align_bytes=64, name="w1_bf", tag="x_two_words")
         w1_dealt = w1_bf[:].rearrange("p (t m j) -> p m j t", t=PACK, j=PACK)
         for u in range(2):
             nc.scalar.copy(w1_dealt[:, u * (P // 2) : (u + 1) * (P // 2)], w1_raw[u][:].rearrange("p j (m t) -> p m j t", t=PACK))
@@ -129,11 +122,18 @@ def tile_picked_jkeyghopmhopnglse_none_p_kernel(tc, x_words, x_scales, w1, d_wor
                     key_scales[2 * odd + r : P : 32, :].bitcast(I32),
                     key_bytes_dealt[LIST_ROWS * odd + r : P : 32, :].bitcast(I32),
                 )
+        gk_sb = keep.tile([P, PACK], F32, name="gk_sb")
+        nc.sync.dma_start(gk_sb[:], gk.rearrange("(p t) o -> p (t o)", t=PACK))
+        n3_sb = load_list(n3, "n3_sb")
+        n4_sb = load_list(n4, "n4_sb")
+        n2_sb = load_list(n2, "n2_sb")
+        n5_sb = load_list(n5, "n5_sb")
+
         w_raw = keep.tile([P, 2 * PACK * N], F32, name="w_raw", tag="dealt_w_raw")
         w3_raw, w2_raw = w_raw[:, : PACK * N], w_raw[:, PACK * N :]
         nc.sync.dma_start(w3_raw, w3.rearrange("(p j) c -> p (j c)", j=PACK))
         nc.sync.dma_start(w2_raw, w2.rearrange("(p j) c -> p (j c)", j=PACK))
-        x_two = gather_codes(x_table, x_bytes, two_sb, "x_two")
+        x_two = gather_codes(x_table, x_bytes, two_sb, "x_two", "x_two_words")
         key_words = keep.tile([P, H], U32, name="key_words")
         nc.vector.tensor_copy(key_words[:], d_table[:].indirect(kidx_sb[:]))
         key_codes = keep.tile([P, H], U32, align_bytes=64, name="key_codes", tag="key_codes")
@@ -160,7 +160,7 @@ def tile_picked_jkeyghopmhopnglse_none_p_kernel(tc, x_words, x_scales, w1, d_wor
                 nc.scalar.activation(wide[t][:, S + first : S + first + count], tile[:].indirect(entries(n1_sb, first, count)), ACT.Copy)
             y.append(tile)
 
-        num = keep.tile([P, PACK * S], F32, name="num")
+        num = keep.tile([P, PACK * S], F32, name="num", tag="num_members")
         size = keep.tile([P, PACK * S], F32, name="size", tag="size_recip")
         s = keep.tile([P, PACK * S], F32, name="s", tag="s_mx")
         plane = [slice(t * S, (t + 1) * S) for t in range(PACK)]
@@ -181,7 +181,7 @@ def tile_picked_jkeyghopmhopnglse_none_p_kernel(tc, x_words, x_scales, w1, d_wor
         for t in range(PACK):
             nc.scalar.activation(recip[:, t * S : (t + 1) * S], wide[t][:].indirect(n4_sb[:]), ACT.Exp, scale=-1.0)
 
-        st = keep.tile([P, PACK * S], F32, name="st")
+        st = keep.tile([P, PACK * S], F32, name="st", tag="st_members")
         mx = keep.tile([P, PACK * S], F32, name="mx", tag="s_mx")
         for t in range(PACK):
             nc.vector.tensor_tensor(mx[:, plane[t]], wide[t][:, S : 3 * S : 2], wide[t][:, S + 1 : 3 * S : 2], ALU.max)
@@ -204,10 +204,14 @@ def tile_picked_jkeyghopmhopnglse_none_p_kernel(tc, x_words, x_scales, w1, d_wor
         for t in range(N // P):
             product(h[t][:], w3_q, slice(t * P, (t + 1) * P), z2_q, True, False)
 
-        for first, count in ((0, 256), (256, 128), (384, 128)):
+        for first, count in ((0, 128), (128, 256), (384, 128)):
             other = keep.tile([P, PACK * count], F32, name="other%d" % first)
             for t in range(PACK):
-                nc.scalar.activation(other[:, t * count : (t + 1) * count], st[:, plane[t]].indirect(entries(n2_sb, first, count)), ACT.Copy)
+                looked_up = st[:, plane[t]].indirect(entries(n2_sb, first, count))
+                if first == 0:
+                    nc.vector.tensor_copy(other[:, t * count : (t + 1) * count], looked_up)
+                else:
+                    nc.scalar.activation(other[:, t * count : (t + 1) * count], looked_up, ACT.Copy)
             z_bf = keep.tile([P, PACK * count], BF16, align_bytes=64, name="z_bf%d" % first)
             nc.vector.tensor_tensor(woven(z_bf[:]), by_lines(st[:])[:, first // PACK : (first + count) // PACK], by_lines(other[:]), ALU.max)
             z_q = quantize(z_bf[:], "z%d" % first)
@@ -217,39 +221,39 @@ def tile_picked_jkeyghopmhopnglse_none_p_kernel(tc, x_words, x_scales, w1, d_wor
         for t in range(N // P):
             nc.scalar.activation(wide[t][:, :S], h[t][:], ACT.Exp)
 
-        units = [(0, 0, S), (1, 0, S), (2, 0, S), (3, 0, HALF), (3, HALF, HALF)]
-        members = {}
-        totals = {}
+        units = [(0, 0, S), (1, 0, S), (2, 0, S), (3, 0, 256), (3, 256, 256)]
+        vector_share = {0: 1408, 1: 640, 2: 640, 3: 0}
+        spent = ("size_recip", "s_mx", "num_members", "st_members")
+        members = [keep.tile([P, 4 * S], F32, name="members%d" % t, tag=spent[t]) for t in range(N // P)]
+        pairs = [keep.tile([P, S, 2], F32, name="pairs%d" % t) for t in range(N // P)]
+        part = [keep.tile([P, S], F32, name="part%d" % t) for t in range(N // P)]
+        total = [keep.tile([P, S], F32, name="total%d" % t) for t in range(N // P)]
 
         def fetch(t, first, count):
-            tile = ring.tile([P, 4 * count], F32, name="members")
-            cut = 4 * count * 3 // 8
-            nc.vector.tensor_copy(tile[:, :cut], wide[t][:].indirect(entries(n5_sb, 4 * first, cut)))
-            nc.scalar.activation(tile[:, cut:], wide[t][:].indirect(entries(n5_sb, 4 * first + cut, 4 * count - cut)), ACT.Copy)
-            members[t, first] = tile
+            begin, cut, end = 4 * first, 4 * first + vector_share[t], 4 * (first + count)
+            if cut > begin:
+                nc.vector.tensor_copy(members[t][:, begin:cut], wide[t][:].indirect(entries(n5_sb, begin, cut - begin)))
+            nc.scalar.activation(members[t][:, cut:end], wide[t][:].indirect(entries(n5_sb, cut, end - cut)), ACT.Copy)
 
         def add_up(t, first, count):
-            quads = members[t, first][:].rearrange("p (j e) -> p j e", e=4)
-            pairs = ring.tile([P, count, 2], F32, name="pairs", bufs=2)
-            nc.vector.tensor_tensor(pairs[:], quads[:, :, 0:2], quads[:, :, 2:4], ALU.add)
-            part = ring.tile([P, count], F32, name="part", bufs=2)
-            nc.vector.tensor_tensor(part[:], pairs[:, :, 0], wide[t][:, first : first + count], ALU.add)
-            total = ring.tile([P, count], F32, name="total", bufs=2)
-            nc.vector.tensor_tensor(total[:], pairs[:, :, 1], part[:], ALU.add)
-            totals[t, first] = total
+            halves = (slice(first, first + count // 2), slice(first + count // 2, first + count))
+            quads = members[t][:].rearrange("p (j e) -> p j e", e=4)
+            for cols in halves:
+                nc.vector.tensor_tensor(pairs[t][:, cols], quads[:, cols, 0:2], quads[:, cols, 2:4], ALU.add)
+            for cols in halves:
+                nc.vector.tensor_tensor(part[t][:, cols], pairs[t][:, cols, 0], wide[t][:, cols], ALU.add)
+            for cols in halves:
+                nc.vector.tensor_tensor(total[t][:, cols], pairs[t][:, cols, 1], part[t][:, cols], ALU.add)
 
         def finish(t, first, count):
             cols = slice(first, first + count)
-            logs = ring.tile([P, count], F32, name="logs", bufs=2)
-            nc.scalar.activation(logs[:], totals[t, first][:], ACT.Ln)
-            result = ring.tile([P, count], F32, name="result", bufs=2)
-            nc.vector.tensor_tensor(result[:], logs[:], h[t][:, cols], ALU.subtract)
-            nc.sync.dma_start(out[t * P : (t + 1) * P, cols], result[:])
+            nc.scalar.activation(part[t][:, cols], total[t][:, cols], ACT.Ln)
+            nc.vector.tensor_tensor(total[t][:, cols], part[t][:, cols], h[t][:, cols], ALU.subtract)
+            nc.sync.dma_start(out[t * P : (t + 1) * P, cols], total[t][:, cols])
 
-        for step in range(len(units) + 2):
-            if step < len(units):
-                fetch(*units[step])
-            if 1 <= step <= len(units):
-                add_up(*units[step - 1])
-            if step >= 2:
-                finish(*units[step - 2])
+        for unit in units:
+            fetch(*unit)
+        for unit in units:
+            add_up(*unit)
+        for unit in units:
+            finish(*unit)

@@ -1,6 +1,7 @@
 from contextlib import ExitStack
 
 import concourse.mybir as mybir
+from concourse.masks import make_identity
 
 K, T, S, N, H, G = 512, 1024, 512, 512, 512, 2048
 FLOPS = 4 * 2 * 512 * 512 * 512
@@ -65,7 +66,10 @@ def tile_picked_jkeyghopmhopnglse_none_p_kernel(tc, x_words, x_scales, w1, d_wor
         d_bytes = keep.tile([P, G], U8, name="d_bytes")
         key_scales = keep.tile([P, H], U8, align_bytes=64, name="key_scales")
         for tile in (x_bytes, d_bytes, key_scales):
-            nc.vector.memset(tile[:].bitcast(I32), 0)
+            nc.gpsimd.memset(tile[:].bitcast(I32), 0)
+
+        identity = keep.tile([P, P], F32, name="identity")
+        make_identity(nc, identity[:])
 
         offs_sb = load_list(offs, "offs_sb")
         x_table = keep.tile([P, T], U32, name="x_table")
@@ -99,7 +103,7 @@ def tile_picked_jkeyghopmhopnglse_none_p_kernel(tc, x_words, x_scales, w1, d_wor
         w1_dealt = w1_bf[:].rearrange("p (t m j) -> p m j t", t=PACK, j=PACK)
         for u in range(2):
             nc.scalar.copy(w1_dealt[:, u * (P // 2) : (u + 1) * (P // 2)], w1_raw[u][:].rearrange("p j (m t) -> p m j t", t=PACK))
-        w1_q = quantize(w1_bf[:], "w1")
+        w1_q = [quantize(w1_bf[:, t * H : (t + 1) * H], "w1_%d" % t) for t in range(PACK)]
 
         gn_neg = keep.tile([P, PACK], F32, name="gn_neg")
         gn_sign = keep.tile([P, PACK], F32, name="gn_sign")
@@ -110,7 +114,7 @@ def tile_picked_jkeyghopmhopnglse_none_p_kernel(tc, x_words, x_scales, w1, d_wor
 
         banks_a = [psum.tile([P, S], F32, name="y_acc%d" % t, tag="bank_a%d" % t) for t in range(PACK)]
         for t in range(PACK):
-            product(banks_a[t][:], w1_q, slice(t * P, (t + 1) * P), x_idx, True, True)
+            product(banks_a[t][:], w1_q[t], slice(0, P), x_idx, True, True)
 
         key_bytes = keep.tile([P, H], U8, name="key_bytes")
         nc.vector.tensor_copy(key_bytes[:], d_bytes[:].indirect(kidx_sb[:]))
@@ -197,42 +201,57 @@ def tile_picked_jkeyghopmhopnglse_none_p_kernel(tc, x_words, x_scales, w1, d_wor
         w3_q = quantize(w3_bf[:], "w3")
         w2_q = quantize(w2_bf[:], "w2")
 
-        z2_bf = keep.tile([P, PACK * S], BF16, align_bytes=64, name="z2_bf")
-        nc.vector.tensor_tensor(woven(z2_bf[:]), by_lines(num[:]), by_lines(recip[:]), ALU.mult)
-        z2_q = quantize(z2_bf[:], "z2")
-        h = [psum.tile([P, S], F32, name="h_acc%d" % t, tag="bank_a%d" % t) for t in range(N // P)]
-        for t in range(N // P):
-            product(h[t][:], w3_q, slice(t * P, (t + 1) * P), z2_q, True, False)
-
-        for first, count in ((0, 128), (128, 256), (384, 128)):
+        def make_z(first, count, gather):
             other = keep.tile([P, PACK * count], F32, name="other%d" % first)
             for t in range(PACK):
-                looked_up = st[:, plane[t]].indirect(entries(n2_sb, first, count))
-                if first == 0:
-                    nc.vector.tensor_copy(other[:, t * count : (t + 1) * count], looked_up)
-                else:
-                    nc.scalar.activation(other[:, t * count : (t + 1) * count], looked_up, ACT.Copy)
+                gather(other[:, t * count : (t + 1) * count], st[:, plane[t]].indirect(entries(n2_sb, first, count)))
             z_bf = keep.tile([P, PACK * count], BF16, align_bytes=64, name="z_bf%d" % first)
             nc.vector.tensor_tensor(woven(z_bf[:]), by_lines(st[:])[:, first // PACK : (first + count) // PACK], by_lines(other[:]), ALU.max)
-            z_q = quantize(z_bf[:], "z%d" % first)
+            return quantize(z_bf[:], "z%d" % first)
+
+        def scalar_gather(dst, src):
+            nc.scalar.activation(dst, src, ACT.Copy)
+
+        def make_z2(first, count):
+            z2_bf = keep.tile([P, PACK * count], BF16, align_bytes=64, name="z2_bf%d" % first)
+            lines = slice(first // PACK, (first + count) // PACK)
+            nc.vector.tensor_tensor(woven(z2_bf[:]), by_lines(num[:])[:, lines], by_lines(recip[:])[:, lines], ALU.mult)
+            return quantize(z2_bf[:], "z2_%d" % first)
+
+        h = [psum.tile([P, S], F32, name="h_acc%d" % t, tag="bank_a%d" % t) for t in range(N // P)]
+
+        def add_to_h(weights, codes, first, count, start, stop):
             for t in range(N // P):
-                product(h[t][:, first : first + count], w2_q, slice(t * P, (t + 1) * P), z_q, False, first + count == S)
+                product(h[t][:, first : first + count], weights, slice(t * P, (t + 1) * P), codes, start, stop)
+
+        chunks = ((0, 128), (128, 256), (384, 128))
+        add_to_h(w2_q, make_z(*chunks[0], nc.vector.tensor_copy), *chunks[0], True, False)
+        for chunk in chunks:
+            add_to_h(w3_q, make_z2(*chunk), *chunk, False, False)
+        for chunk in chunks[1:]:
+            add_to_h(w2_q, make_z(*chunk, scalar_gather), *chunk, False, chunk == chunks[-1])
 
         for t in range(N // P):
             nc.scalar.activation(wide[t][:, :S], h[t][:], ACT.Exp)
 
         units = [(0, 0, S), (1, 0, S), (2, 0, S), (3, 0, 256), (3, 256, 256)]
-        vector_share = {0: 1408, 1: 640, 2: 640, 3: 0}
+        vector_share = {0: 1408, 1: 1280, 2: 1152, 3: 0}
+        turned_tiles = 2
         spent = ("size_recip", "s_mx", "num_members", "st_members")
         members = [keep.tile([P, 4 * S], F32, name="members%d" % t, tag=spent[t]) for t in range(N // P)]
-        pairs = [keep.tile([P, S, 2], F32, name="pairs%d" % t) for t in range(N // P)]
+        pairs = {t: keep.tile([P, S, 2], F32, name="pairs%d" % t) for t in range(turned_tiles, N // P)}
+        h_sb = [keep.tile([P, S], F32, name="h_sb%d" % t) for t in range(turned_tiles)]
+        turned = [psum.tile([P, S], F32, name="turned%d" % t, tag="bank_b%d" % t) for t in range(turned_tiles)]
+        logs = [psum.tile([P, S], F32, name="logs%d" % t, tag="bank_b%d" % (turned_tiles + t)) for t in range(turned_tiles)]
         part = [keep.tile([P, S], F32, name="part%d" % t) for t in range(N // P)]
         total = [keep.tile([P, S], F32, name="total%d" % t) for t in range(N // P)]
 
         def fetch(t, first, count):
             begin, cut, end = 4 * first, 4 * first + vector_share[t], 4 * (first + count)
-            if cut > begin:
-                nc.vector.tensor_copy(members[t][:, begin:cut], wide[t][:].indirect(entries(n5_sb, begin, cut - begin)))
+            piece = 4 * P if t == 0 else 4 * S
+            for low in range(begin, cut, piece):
+                high = min(low + piece, cut)
+                nc.vector.tensor_copy(members[t][:, low:high], wide[t][:].indirect(entries(n5_sb, low, high - low)))
             nc.scalar.activation(members[t][:, cut:end], wide[t][:].indirect(entries(n5_sb, cut, end - cut)), ACT.Copy)
 
         def add_up(t, first, count):
@@ -251,9 +270,27 @@ def tile_picked_jkeyghopmhopnglse_none_p_kernel(tc, x_words, x_scales, w1, d_wor
             nc.vector.tensor_tensor(total[t][:, cols], part[t][:, cols], h[t][:, cols], ALU.subtract)
             nc.sync.dma_start(out[t * P : (t + 1) * P, cols], total[t][:, cols])
 
+        def add_up_turned(t):
+            nc.vector.tensor_copy(h_sb[t][:], h[t][:])
+            for b in range(S // P):
+                terms = [members[t][:, 4 * P * b + e : 4 * P * (b + 1) : 4] for e in range(4)] + [wide[t][:, P * b : P * (b + 1)]]
+                for e, term in enumerate(terms):
+                    nc.tensor.matmul(turned[t][:, P * b : P * (b + 1)], term, identity[:], start=e == 0, stop=e == len(terms) - 1, is_transpose=True)
+
+        def finish_turned(t):
+            nc.scalar.activation(part[t][:], turned[t][:], ACT.Ln)
+            for b in range(S // P):
+                nc.tensor.transpose(logs[t][:, P * b : P * (b + 1)], part[t][:, P * b : P * (b + 1)], identity[:])
+            nc.vector.tensor_tensor(total[t][:], logs[t][:], h_sb[t][:], ALU.subtract)
+            nc.sync.dma_start(out[t * P : (t + 1) * P, :], total[t][:])
+
         for unit in units:
             fetch(*unit)
-        for unit in units:
+        for t in range(turned_tiles):
+            add_up_turned(t)
+        for unit in units[turned_tiles:]:
             add_up(*unit)
-        for unit in units:
+        for t in range(turned_tiles):
+            finish_turned(t)
+        for unit in units[turned_tiles:]:
             finish(*unit)

@@ -3,7 +3,7 @@ from contextlib import ExitStack
 import concourse.mybir as mybir
 from concourse.masks import make_identity
 
-K, T, S, N, H, G = 512, 1024, 512, 512, 512, 2048
+T, S, N, H, G = 1024, 512, 512, 512, 2048
 FLOPS = 4 * 2 * 512 * 512 * 512
 
 F32 = mybir.dt.float32
@@ -18,11 +18,21 @@ ACT = mybir.ActivationFunctionType
 
 P = 128
 PACK = 4
+QUADRANT = 32
 LIST_ROWS = 16
 HALF = S // 2
+MEMBERS = 4
+OUT_TILES = N // P
+
+N1_PIECES = ((0, 352), (352, 352), (704, 320))
+Z_CHUNKS = ((0, 128), (128, 256), (384, 128))
+TURNED_TILES = 2
+VECTOR_ENTRIES = (1408, 1280, 1152, 0)
 
 
-def tile_picked_jkeyghopmhopnglse_none_p_kernel(tc, x_words, x_scales, w1, d_words, d_scales, gn, gk, w2, w3, offs, kidx, two, n1, n2, n3, n4, n5, out):
+def tile_picked_jkeyghopmhopnglse_none_p_kernel(
+    tc, x_words, x_scales, w1, d_words, d_scales, gn, gk, w2, w3, offs, kidx, two, n1, n2, n3, n4, n5, out
+):
     nc = tc.nc
 
     with ExitStack() as ctx:
@@ -62,6 +72,9 @@ def tile_picked_jkeyghopmhopnglse_none_p_kernel(tc, x_words, x_scales, w1, d_wor
                 stop=stop,
             )
 
+        def scalar_gather(dst, src):
+            nc.scalar.activation(dst, src, ACT.Copy)
+
         x_bytes = keep.tile([P, T], U8, name="x_bytes")
         d_bytes = keep.tile([P, G], U8, name="d_bytes")
         key_scales = keep.tile([P, H], U8, align_bytes=64, name="key_scales")
@@ -74,35 +87,38 @@ def tile_picked_jkeyghopmhopnglse_none_p_kernel(tc, x_words, x_scales, w1, d_wor
         offs_sb = load_list(offs, "offs_sb")
         x_table = keep.tile([P, T], U32, name="x_table")
         nc.sync.dma_start(x_table[:].bitcast(I32), x_words[0].rearrange("p n t -> p (n t)").bitcast(I32))
-        for q in range(4):
-            nc.sync.dma_start(x_bytes[32 * q : 32 * q + 4, :].bitcast(I32), x_scales[0, 4 * q : 4 * q + 4, :].bitcast(I32))
+        for q in range(P // QUADRANT):
+            nc.sync.dma_start(x_bytes[QUADRANT * q : QUADRANT * q + 4, :].bitcast(I32), x_scales[0, 4 * q : 4 * q + 4, :].bitcast(I32))
         w1_raw = []
         for u in range(2):
             raw = keep.tile([P, PACK, HALF], F32, name="w1_raw%d" % u, tag=("w1_raw", "dealt_w_raw")[u])
             nc.sync.dma_start(raw[:], w1[:, u * HALF : (u + 1) * HALF].rearrange("(p j) c -> p j c", j=PACK))
             w1_raw.append(raw)
+        gn_sb = keep.tile([P, PACK], F32, name="gn_sb")
+        nc.sync.dma_start(gn_sb[:], gn.rearrange("(p t) o -> p (t o)", t=PACK))
         kidx_sb = load_list(kidx, "kidx_sb")
         for r in range(2):
             nc.sync.dma_start(d_bytes[r:P:LIST_ROWS, :].bitcast(I32), d_scales[0, r:16:2, :].bitcast(I32))
-        two_sb = load_list(two, "two_sb")
-        gn_sb = keep.tile([P, PACK], F32, name="gn_sb")
-        nc.sync.dma_start(gn_sb[:], gn.rearrange("(p t) o -> p (t o)", t=PACK))
         n1_sb = load_list(n1, "n1_sb")
+        two_sb = load_list(two, "two_sb")
         d_table = keep.tile([P, G], U32, name="d_table")
         nc.sync.dma_start(d_table[:].bitcast(I32), d_words[0].rearrange("p n t -> p (n t)").bitcast(I32))
 
-        def gather_codes(table, table_bytes, offsets, name, words_tag):
+        def gather_tokens(offsets, name, words_tag):
             words = keep.tile([P, S], U32, align_bytes=64, name=name + "_words", tag=words_tag)
             scales = keep.tile([P, S], U8, align_bytes=64, name=name + "_bytes", tag="token_bytes")
-            nc.vector.tensor_copy(words[:], table[:].indirect(offsets[:]))
-            nc.vector.tensor_copy(scales[:], table_bytes[:].indirect(offsets[:]))
+            nc.vector.tensor_copy(words[:], x_table[:].indirect(offsets[:]))
+            nc.vector.tensor_copy(scales[:], x_bytes[:].indirect(offsets[:]))
             return words, scales
 
-        x_idx = gather_codes(x_table, x_bytes, offs_sb, "x_idx", "x_idx_words")
+        x_idx = gather_tokens(offs_sb, "x_idx", "x_idx_words")
         w1_bf = keep.tile([P, PACK * H], BF16, align_bytes=64, name="w1_bf", tag="x_two_words")
         w1_dealt = w1_bf[:].rearrange("p (t m j) -> p m j t", t=PACK, j=PACK)
-        for u in range(2):
-            nc.scalar.copy(w1_dealt[:, u * (P // 2) : (u + 1) * (P // 2)], w1_raw[u][:].rearrange("p j (m t) -> p m j t", t=PACK))
+        w1_lines = [raw[:].rearrange("p j (m t) -> p m j t", t=PACK) for raw in w1_raw]
+        quarter = P // 4
+        nc.scalar.copy(w1_dealt[:, : 2 * quarter], w1_lines[0])
+        nc.scalar.copy(w1_dealt[:, 2 * quarter : 3 * quarter], w1_lines[1][:, :quarter])
+        nc.vector.tensor_copy(w1_dealt[:, 3 * quarter :], w1_lines[1][:, quarter:])
         w1_q = [quantize(w1_bf[:, t * H : (t + 1) * H], "w1_%d" % t) for t in range(PACK)]
 
         gn_neg = keep.tile([P, PACK], F32, name="gn_neg")
@@ -110,11 +126,11 @@ def tile_picked_jkeyghopmhopnglse_none_p_kernel(tc, x_words, x_scales, w1, d_wor
         gn_abs = keep.tile([P, PACK], F32, name="gn_abs")
         nc.gpsimd.tensor_scalar(gn_neg[:], gn_sb[:], 0.0, -2.0, ALU.is_lt, ALU.mult)
         nc.gpsimd.tensor_scalar(gn_sign[:], gn_neg[:], 1.0, 1.0, ALU.mult, ALU.add)
-        nc.gpsimd.tensor_tensor(gn_abs[:], gn_sb[:], gn_sign[:], ALU.mult)
+        nc.scalar.activation(gn_abs[:], gn_sb[:], ACT.Abs)
 
-        banks_a = [psum.tile([P, S], F32, name="y_acc%d" % t, tag="bank_a%d" % t) for t in range(PACK)]
+        y_acc = [psum.tile([P, S], F32, name="y_acc%d" % t, tag="bank_a%d" % t) for t in range(PACK)]
         for t in range(PACK):
-            product(banks_a[t][:], w1_q[t], slice(0, P), x_idx, True, True)
+            product(y_acc[t][:], w1_q[t], slice(0, P), x_idx, True, True)
 
         key_bytes = keep.tile([P, H], U8, name="key_bytes")
         nc.vector.tensor_copy(key_bytes[:], d_bytes[:].indirect(kidx_sb[:]))
@@ -123,8 +139,8 @@ def tile_picked_jkeyghopmhopnglse_none_p_kernel(tc, x_words, x_scales, w1, d_wor
         for odd in range(2):
             for r in range(2):
                 nc.sync.dma_start(
-                    key_scales[2 * odd + r : P : 32, :].bitcast(I32),
-                    key_bytes_dealt[LIST_ROWS * odd + r : P : 32, :].bitcast(I32),
+                    key_scales[2 * odd + r : P : QUADRANT, :].bitcast(I32),
+                    key_bytes_dealt[LIST_ROWS * odd + r : P : QUADRANT, :].bitcast(I32),
                 )
         gk_sb = keep.tile([P, PACK], F32, name="gk_sb")
         nc.sync.dma_start(gk_sb[:], gk.rearrange("(p t) o -> p (t o)", t=PACK))
@@ -137,60 +153,61 @@ def tile_picked_jkeyghopmhopnglse_none_p_kernel(tc, x_words, x_scales, w1, d_wor
         w3_raw, w2_raw = w_raw[:, : PACK * N], w_raw[:, PACK * N :]
         nc.sync.dma_start(w3_raw, w3.rearrange("(p j) c -> p (j c)", j=PACK))
         nc.sync.dma_start(w2_raw, w2.rearrange("(p j) c -> p (j c)", j=PACK))
-        x_two = gather_codes(x_table, x_bytes, two_sb, "x_two", "x_two_words")
+        x_two = gather_tokens(two_sb, "x_two", "x_two_words")
         key_words = keep.tile([P, H], U32, name="key_words")
         nc.vector.tensor_copy(key_words[:], d_table[:].indirect(kidx_sb[:]))
         key_codes = keep.tile([P, H], U32, align_bytes=64, name="key_codes", tag="key_codes")
         nc.vector.tensor_copy(key_codes[:].rearrange("p (t m) -> p m t", t=PACK), key_words[:].rearrange("p (m t) -> p m t", t=PACK))
-        banks_b = [psum.tile([P, S], F32, name="s_acc%d" % t, tag="bank_b%d" % t) for t in range(PACK)]
+        s_acc = [psum.tile([P, S], F32, name="s_acc%d" % t, tag="bank_b%d" % t) for t in range(PACK)]
         for t in range(PACK):
-            product(banks_b[t][:], (key_codes, key_scales), slice(t * P, (t + 1) * P), x_two, True, True)
+            product(s_acc[t][:], (key_codes, key_scales), slice(t * P, (t + 1) * P), x_two, True, True)
 
         gk_zero = keep.tile([P, PACK], F32, name="gk_zero")
         gk_safe = keep.tile([P, PACK], F32, name="gk_safe")
         gk_rec = keep.tile([P, PACK], F32, name="gk_rec")
-        gk_inv = keep.tile([P, PACK], F32, name="gk_inv")
         nc.gpsimd.tensor_scalar(gk_zero[:], gk_sb[:], 0.0, 1.0, ALU.is_equal, ALU.mult)
         nc.gpsimd.tensor_tensor(gk_safe[:], gk_sb[:], gk_zero[:], ALU.add)
+        gk_last = keep.tile([P, 1], F32, name="gk_last")
+        nc.gpsimd.tensor_scalar(gk_last[:], gk_sb[:, PACK - 1 :], 0.0625, 1.0, ALU.mult, ALU.mult)
         nc.vector.reciprocal(gk_rec[:], gk_safe[:])
-        nc.vector.scalar_tensor_tensor(gk_inv[:], gk_rec[:], -1.0, gk_rec[:], ALU.mult, ALU.max)
 
         wide = [keep.tile([P, PACK * S], F32, name="wide%d" % t) for t in range(PACK)]
         y = []
         for t in range(PACK):
             tile = keep.tile([P, S], F32, name="y%d" % t)
-            nc.scalar.activation(tile[:], banks_a[t][:], ACT.Copy, scale=gn_abs[:, t : t + 1])
-            for first, count in ((0, 352), (352, 352), (704, 320)):
-                nc.scalar.activation(wide[t][:, S + first : S + first + count], tile[:].indirect(entries(n1_sb, first, count)), ACT.Copy)
+            nc.scalar.activation(tile[:], y_acc[t][:], ACT.Copy, scale=gn_abs[:, t : t + 1])
+            for first, count in N1_PIECES:
+                scalar_gather(wide[t][:, S + first : S + first + count], tile[:].indirect(entries(n1_sb, first, count)))
             y.append(tile)
 
         num = keep.tile([P, PACK * S], F32, name="num", tag="num_members")
         size = keep.tile([P, PACK * S], F32, name="size", tag="size_recip")
         s = keep.tile([P, PACK * S], F32, name="s", tag="s_mx")
         plane = [slice(t * S, (t + 1) * S) for t in range(PACK)]
-        for t in range(PACK):
-            nc.vector.tensor_scalar(s[:, plane[t]], banks_b[t][:], gk_sb[:, t : t + 1], 0.0625, ALU.mult, ALU.mult)
+        for t in range(PACK - 1):
+            nc.vector.tensor_scalar(s[:, plane[t]], s_acc[t][:], gk_sb[:, t : t + 1], 0.0625, ALU.mult, ALU.mult)
+        nc.scalar.activation(s[:, plane[-1]], s_acc[-1][:], ACT.Copy, scale=gk_last[:])
         for step in range(PACK + 1):
             if step < PACK:
-                for u in range(2):
+                for first in (0, HALF):
                     nc.vector.tensor_copy(
-                        wide[step][:, 3 * S + u * HALF : 3 * S + (u + 1) * HALF], s[:, plane[step]].indirect(entries(n3_sb, u * HALF, HALF))
+                        wide[step][:, 3 * S + first : 3 * S + first + HALF], s[:, plane[step]].indirect(entries(n3_sb, first, HALF))
                     )
             if step >= 1:
                 t = step - 1
                 nc.vector.tensor_tensor(num[:, plane[t]], s[:, plane[t]], wide[t][:, 3 * S :], ALU.subtract)
-                nc.scalar.activation(size[:, plane[t]], num[:, plane[t]], ACT.Abs)
-                nc.scalar.activation(wide[t][:, :S], size[:, plane[t]], ACT.Ln, bias=0.5, scale=gk_inv[:, t : t + 1])
+                nc.scalar.activation(size[:, plane[t]], num[:, plane[t]], ACT.Abs, scale=gk_rec[:, t : t + 1])
+                nc.scalar.activation(wide[t][:, :S], size[:, plane[t]], ACT.Ln, bias=0.5)
         recip = keep.tile([P, PACK * S], F32, name="recip", tag="size_recip")
         for t in range(PACK):
-            nc.scalar.activation(recip[:, t * S : (t + 1) * S], wide[t][:].indirect(n4_sb[:]), ACT.Exp, scale=-1.0)
+            nc.scalar.activation(recip[:, plane[t]], wide[t][:].indirect(n4_sb[:]), ACT.Exp, scale=-1.0)
 
         st = keep.tile([P, PACK * S], F32, name="st", tag="st_members")
         mx = keep.tile([P, PACK * S], F32, name="mx", tag="s_mx")
         for t in range(PACK):
             nc.vector.tensor_tensor(mx[:, plane[t]], wide[t][:, S : 3 * S : 2], wide[t][:, S + 1 : 3 * S : 2], ALU.max)
         for t in range(PACK):
-            nc.vector.tensor_tensor(st[:, t * S : (t + 1) * S], y[t][:], mx[:, plane[t]], ALU.subtract)
+            nc.vector.tensor_tensor(st[:, plane[t]], y[t][:], mx[:, plane[t]], ALU.subtract)
 
         w3_bf = keep.tile([P, PACK * N], BF16, align_bytes=64, name="w3_bf", tag="key_codes")
         nc.vector.tensor_copy(woven(w3_bf[:]), by_lines(w3_raw))
@@ -202,15 +219,13 @@ def tile_picked_jkeyghopmhopnglse_none_p_kernel(tc, x_words, x_scales, w1, d_wor
         w2_q = quantize(w2_bf[:], "w2")
 
         def make_z(first, count, gather):
-            other = keep.tile([P, PACK * count], F32, name="other%d" % first)
+            st_far = keep.tile([P, PACK * count], F32, name="st_far%d" % first)
             for t in range(PACK):
-                gather(other[:, t * count : (t + 1) * count], st[:, plane[t]].indirect(entries(n2_sb, first, count)))
+                gather(st_far[:, t * count : (t + 1) * count], st[:, plane[t]].indirect(entries(n2_sb, first, count)))
             z_bf = keep.tile([P, PACK * count], BF16, align_bytes=64, name="z_bf%d" % first)
-            nc.vector.tensor_tensor(woven(z_bf[:]), by_lines(st[:])[:, first // PACK : (first + count) // PACK], by_lines(other[:]), ALU.max)
+            lines = slice(first // PACK, (first + count) // PACK)
+            nc.vector.tensor_tensor(woven(z_bf[:]), by_lines(st[:])[:, lines], by_lines(st_far[:]), ALU.max)
             return quantize(z_bf[:], "z%d" % first)
-
-        def scalar_gather(dst, src):
-            nc.scalar.activation(dst, src, ACT.Copy)
 
         def make_z2(first, count):
             z2_bf = keep.tile([P, PACK * count], BF16, align_bytes=64, name="z2_bf%d" % first)
@@ -218,79 +233,78 @@ def tile_picked_jkeyghopmhopnglse_none_p_kernel(tc, x_words, x_scales, w1, d_wor
             nc.vector.tensor_tensor(woven(z2_bf[:]), by_lines(num[:])[:, lines], by_lines(recip[:])[:, lines], ALU.mult)
             return quantize(z2_bf[:], "z2_%d" % first)
 
-        h = [psum.tile([P, S], F32, name="h_acc%d" % t, tag="bank_a%d" % t) for t in range(N // P)]
+        h = [psum.tile([P, S], F32, name="h_acc%d" % t, tag="bank_a%d" % t) for t in range(OUT_TILES)]
 
         def add_to_h(weights, codes, first, count, start, stop):
-            for t in range(N // P):
+            for t in range(OUT_TILES):
                 product(h[t][:, first : first + count], weights, slice(t * P, (t + 1) * P), codes, start, stop)
 
-        chunks = ((0, 128), (128, 256), (384, 128))
-        add_to_h(w2_q, make_z(*chunks[0], nc.vector.tensor_copy), *chunks[0], True, False)
-        for chunk in chunks:
+        add_to_h(w2_q, make_z(*Z_CHUNKS[0], nc.vector.tensor_copy), *Z_CHUNKS[0], True, False)
+        for chunk in Z_CHUNKS:
             add_to_h(w3_q, make_z2(*chunk), *chunk, False, False)
-        for chunk in chunks[1:]:
-            add_to_h(w2_q, make_z(*chunk, scalar_gather), *chunk, False, chunk == chunks[-1])
+        for chunk in Z_CHUNKS[1:]:
+            add_to_h(w2_q, make_z(*chunk, scalar_gather), *chunk, False, chunk == Z_CHUNKS[-1])
 
-        for t in range(N // P):
+        h_sb = [keep.tile([P, S], F32, name="h_sb%d" % t) for t in range(TURNED_TILES)]
+        nc.vector.tensor_copy(h_sb[1][:], h[1][:])
+        for t in range(OUT_TILES):
             nc.scalar.activation(wide[t][:, :S], h[t][:], ACT.Exp)
 
-        units = [(0, 0, S), (1, 0, S), (2, 0, S), (3, 0, 256), (3, 256, 256)]
-        vector_share = {0: 1408, 1: 1280, 2: 1152, 3: 0}
-        turned_tiles = 2
+        units = [(t, 0, S) for t in range(OUT_TILES - 1)] + [(OUT_TILES - 1, first, HALF) for first in (0, HALF)]
         spent = ("size_recip", "s_mx", "num_members", "st_members")
-        members = [keep.tile([P, 4 * S], F32, name="members%d" % t, tag=spent[t]) for t in range(N // P)]
-        pairs = {t: keep.tile([P, S, 2], F32, name="pairs%d" % t) for t in range(turned_tiles, N // P)}
-        h_sb = [keep.tile([P, S], F32, name="h_sb%d" % t) for t in range(turned_tiles)]
-        turned = [psum.tile([P, S], F32, name="turned%d" % t, tag="bank_b%d" % t) for t in range(turned_tiles)]
-        logs = [psum.tile([P, S], F32, name="logs%d" % t, tag="bank_b%d" % (turned_tiles + t)) for t in range(turned_tiles)]
-        part = [keep.tile([P, S], F32, name="part%d" % t) for t in range(N // P)]
-        total = [keep.tile([P, S], F32, name="total%d" % t) for t in range(N // P)]
+        members = [keep.tile([P, MEMBERS * S], F32, name="members%d" % t, tag=spent[t]) for t in range(OUT_TILES)]
+        pairs = {t: keep.tile([P, S, 2], F32, name="pairs%d" % t) for t in range(TURNED_TILES, OUT_TILES)}
+        turned = [psum.tile([P, S], F32, name="turned%d" % t, tag="bank_b%d" % t) for t in range(TURNED_TILES)]
+        logs = [psum.tile([P, S], F32, name="logs%d" % t, tag="bank_b%d" % (TURNED_TILES + t)) for t in range(TURNED_TILES)]
+        work_a = [keep.tile([P, S], F32, name="work_a%d" % t) for t in range(OUT_TILES)]
+        work_b = [keep.tile([P, S], F32, name="work_b%d" % t) for t in range(OUT_TILES)]
 
         def fetch(t, first, count):
-            begin, cut, end = 4 * first, 4 * first + vector_share[t], 4 * (first + count)
-            piece = 4 * P if t == 0 else 4 * S
+            begin, cut, end = MEMBERS * first, MEMBERS * first + VECTOR_ENTRIES[t], MEMBERS * (first + count)
+            piece = MEMBERS * P if t == 0 else MEMBERS * S
             for low in range(begin, cut, piece):
                 high = min(low + piece, cut)
                 nc.vector.tensor_copy(members[t][:, low:high], wide[t][:].indirect(entries(n5_sb, low, high - low)))
-            nc.scalar.activation(members[t][:, cut:end], wide[t][:].indirect(entries(n5_sb, cut, end - cut)), ACT.Copy)
+            scalar_gather(members[t][:, cut:end], wide[t][:].indirect(entries(n5_sb, cut, end - cut)))
 
         def add_up(t, first, count):
             halves = (slice(first, first + count // 2), slice(first + count // 2, first + count))
-            quads = members[t][:].rearrange("p (j e) -> p j e", e=4)
+            quads = members[t][:].rearrange("p (j e) -> p j e", e=MEMBERS)
             for cols in halves:
                 nc.vector.tensor_tensor(pairs[t][:, cols], quads[:, cols, 0:2], quads[:, cols, 2:4], ALU.add)
             for cols in halves:
-                nc.vector.tensor_tensor(part[t][:, cols], pairs[t][:, cols, 0], wide[t][:, cols], ALU.add)
+                nc.vector.tensor_tensor(work_a[t][:, cols], pairs[t][:, cols, 0], wide[t][:, cols], ALU.add)
             for cols in halves:
-                nc.vector.tensor_tensor(total[t][:, cols], pairs[t][:, cols, 1], part[t][:, cols], ALU.add)
+                nc.vector.tensor_tensor(work_b[t][:, cols], pairs[t][:, cols, 1], work_a[t][:, cols], ALU.add)
 
         def finish(t, first, count):
             cols = slice(first, first + count)
-            nc.scalar.activation(part[t][:, cols], total[t][:, cols], ACT.Ln)
-            nc.vector.tensor_tensor(total[t][:, cols], part[t][:, cols], h[t][:, cols], ALU.subtract)
-            nc.sync.dma_start(out[t * P : (t + 1) * P, cols], total[t][:, cols])
+            nc.scalar.activation(work_a[t][:, cols], work_b[t][:, cols], ACT.Ln)
+            nc.vector.tensor_tensor(work_b[t][:, cols], work_a[t][:, cols], h[t][:, cols], ALU.subtract)
+            nc.sync.dma_start(out[t * P : (t + 1) * P, cols], work_b[t][:, cols])
 
         def add_up_turned(t):
-            nc.vector.tensor_copy(h_sb[t][:], h[t][:])
             for b in range(S // P):
-                terms = [members[t][:, 4 * P * b + e : 4 * P * (b + 1) : 4] for e in range(4)] + [wide[t][:, P * b : P * (b + 1)]]
+                terms = [members[t][:, MEMBERS * P * b + e : MEMBERS * P * (b + 1) : MEMBERS] for e in range(MEMBERS)]
+                terms.append(wide[t][:, P * b : P * (b + 1)])
                 for e, term in enumerate(terms):
-                    nc.tensor.matmul(turned[t][:, P * b : P * (b + 1)], term, identity[:], start=e == 0, stop=e == len(terms) - 1, is_transpose=True)
+                    nc.tensor.matmul(turned[t][:, P * b : P * (b + 1)], term, identity[:], start=e == 0, stop=e == MEMBERS, is_transpose=True)
 
         def finish_turned(t):
-            nc.scalar.activation(part[t][:], turned[t][:], ACT.Ln)
+            nc.scalar.activation(work_a[t][:], turned[t][:], ACT.Ln)
             for b in range(S // P):
-                nc.tensor.transpose(logs[t][:, P * b : P * (b + 1)], part[t][:, P * b : P * (b + 1)], identity[:])
-            nc.vector.tensor_tensor(total[t][:], logs[t][:], h_sb[t][:], ALU.subtract)
-            nc.sync.dma_start(out[t * P : (t + 1) * P, :], total[t][:])
+                nc.tensor.transpose(logs[t][:, P * b : P * (b + 1)], work_a[t][:, P * b : P * (b + 1)], identity[:])
+            nc.vector.tensor_tensor(work_b[t][:], logs[t][:], h_sb[t][:], ALU.subtract)
+            nc.sync.dma_start(out[t * P : (t + 1) * P, :], work_b[t][:])
 
         for unit in units:
             fetch(*unit)
-        for t in range(turned_tiles):
+        nc.vector.tensor_copy(h_sb[0][:], h[0][:])
+        for t in range(TURNED_TILES):
             add_up_turned(t)
-        for unit in units[turned_tiles:]:
+        for unit in units[TURNED_TILES:]:
             add_up(*unit)
-        for t in range(turned_tiles):
+        for t in range(TURNED_TILES):
             finish_turned(t)
-        for unit in units[turned_tiles:]:
+        for unit in units[TURNED_TILES:]:
             finish(*unit)

from contextlib import ExitStack

import concourse.mybir as mybir
from concourse.masks import make_identity

T, S, N, H, G = 1024, 512, 512, 512, 2048
FLOPS = 4 * 2 * 512 * 512 * 512

F32 = mybir.dt.float32
BF16 = mybir.dt.bfloat16
I32 = mybir.dt.int32
U32 = mybir.dt.uint32
U16 = mybir.dt.uint16
U8 = mybir.dt.uint8
FP8X4 = mybir.dt.float8_e4m3fn_x4
ALU = mybir.AluOpType
ACT = mybir.ActivationFunctionType

P = 128
PACK = 4
QUADRANT = 32
LIST_ROWS = 16
HALF = S // 2
MEMBERS = 4
OUT_TILES = N // P

N1_PIECES = ((0, 352), (352, 352), (704, 320))
Z_CHUNKS = ((0, 128), (128, 256), (384, 128))
TURNED_TILES = 2
VECTOR_ENTRIES = (1408, 1280, 1152, 0)


def tile_picked_jkeyghopmhopnglse_none_p_kernel(
    tc, x_words, x_scales, w1, d_words, d_scales, gn, gk, w2, w3, offs, kidx, two, n1, n2, n3, n4, n5, out
):
    nc = tc.nc

    with ExitStack() as ctx:
        lists = ctx.enter_context(tc.tile_pool(name="lists", bufs=1))
        keep = ctx.enter_context(tc.tile_pool(name="keep", bufs=1))
        psum = ctx.enter_context(tc.psum_pool(name="psum", bufs=1))

        def load_list(src, name):
            tile = lists.tile(list(src.shape), U16, name=name)
            nc.sync.dma_start(tile[:], src)
            return tile

        def entries(tile, first, count):
            return tile[:, first // LIST_ROWS : (first + count) // LIST_ROWS]

        def by_lines(ap):
            return ap.rearrange("p (t c i) -> p c t i", t=PACK, i=PACK)

        def woven(ap):
            return ap.rearrange("p (c i t) -> p c t i", t=PACK, i=PACK)

        def quantize(values, name):
            width = values.shape[1] // PACK
            codes = keep.tile([P, width], U32, align_bytes=64, name=name + "_codes")
            scales = keep.tile([P, width], U8, align_bytes=64, name=name + "_scales")
            nc.vector.quantize_mx(out=codes[:].bitcast(FP8X4), scales=scales[:], in_=values)
            return codes, scales

        def product(acc, left, cols, right, start, stop):
            nc.tensor.matmul_mx(
                out=acc,
                lhsT=left[0][:, cols].bitcast(FP8X4),
                lhsT_scale=left[1][:, cols],
                rhs=right[0][:].bitcast(FP8X4),
                rhs_scale=right[1][:],
                start=start,
                stop=stop,
            )

        def scalar_gather(dst, src):
            nc.scalar.activation(dst, src, ACT.Copy)

        x_bytes = keep.tile([P, T], U8, name="x_bytes")
        d_bytes = keep.tile([P, G], U8, name="d_bytes")
        key_scales = keep.tile([P, H], U8, align_bytes=64, name="key_scales")
        for tile in (x_bytes, d_bytes, key_scales):
            nc.gpsimd.memset(tile[:].bitcast(I32), 0)

        identity = keep.tile([P, P], F32, name="identity")
        make_identity(nc, identity[:])

        offs_sb = load_list(offs, "offs_sb")
        x_table = keep.tile([P, T], U32, name="x_table")
        nc.sync.dma_start(x_table[:].bitcast(I32), x_words[0].rearrange("p n t -> p (n t)").bitcast(I32))
        for q in range(P // QUADRANT):
            nc.sync.dma_start(x_bytes[QUADRANT * q : QUADRANT * q + 4, :].bitcast(I32), x_scales[0, 4 * q : 4 * q + 4, :].bitcast(I32))
        w1_raw = []
        for u in range(2):
            raw = keep.tile([P, PACK, HALF], F32, name="w1_raw%d" % u, tag=("w1_raw", "dealt_w_raw")[u])
            nc.sync.dma_start(raw[:], w1[:, u * HALF : (u + 1) * HALF].rearrange("(p j) c -> p j c", j=PACK))
            w1_raw.append(raw)
        gn_sb = keep.tile([P, PACK], F32, name="gn_sb")
        nc.sync.dma_start(gn_sb[:], gn.rearrange("(p t) o -> p (t o)", t=PACK))
        kidx_sb = load_list(kidx, "kidx_sb")
        for r in range(2):
            nc.sync.dma_start(d_bytes[r:P:LIST_ROWS, :].bitcast(I32), d_scales[0, r:16:2, :].bitcast(I32))
        n1_sb = load_list(n1, "n1_sb")
        two_sb = load_list(two, "two_sb")
        d_table = keep.tile([P, G], U32, name="d_table")
        nc.sync.dma_start(d_table[:].bitcast(I32), d_words[0].rearrange("p n t -> p (n t)").bitcast(I32))

        def gather_tokens(offsets, name, words_tag):
            words = keep.tile([P, S], U32, align_bytes=64, name=name + "_words", tag=words_tag)
            scales = keep.tile([P, S], U8, align_bytes=64, name=name + "_bytes", tag="token_bytes")
            nc.vector.tensor_copy(words[:], x_table[:].indirect(offsets[:]))
            nc.vector.tensor_copy(scales[:], x_bytes[:].indirect(offsets[:]))
            return words, scales

        x_idx = gather_tokens(offs_sb, "x_idx", "x_idx_words")
        w1_bf = keep.tile([P, PACK * H], BF16, align_bytes=64, name="w1_bf", tag="x_two_words")
        w1_dealt = w1_bf[:].rearrange("p (t m j) -> p m j t", t=PACK, j=PACK)
        w1_lines = [raw[:].rearrange("p j (m t) -> p m j t", t=PACK) for raw in w1_raw]
        quarter = P // 4
        nc.scalar.copy(w1_dealt[:, : 2 * quarter], w1_lines[0])
        nc.scalar.copy(w1_dealt[:, 2 * quarter : 3 * quarter], w1_lines[1][:, :quarter])
        nc.vector.tensor_copy(w1_dealt[:, 3 * quarter :], w1_lines[1][:, quarter:])
        w1_q = [quantize(w1_bf[:, t * H : (t + 1) * H], "w1_%d" % t) for t in range(PACK)]

        gn_neg = keep.tile([P, PACK], F32, name="gn_neg")
        gn_sign = keep.tile([P, PACK], F32, name="gn_sign")
        gn_abs = keep.tile([P, PACK], F32, name="gn_abs")
        nc.gpsimd.tensor_scalar(gn_neg[:], gn_sb[:], 0.0, -2.0, ALU.is_lt, ALU.mult)
        nc.gpsimd.tensor_scalar(gn_sign[:], gn_neg[:], 1.0, 1.0, ALU.mult, ALU.add)
        nc.scalar.activation(gn_abs[:], gn_sb[:], ACT.Abs)

        y_acc = [psum.tile([P, S], F32, name="y_acc%d" % t, tag="bank_a%d" % t) for t in range(PACK)]
        for t in range(PACK):
            product(y_acc[t][:], w1_q[t], slice(0, P), x_idx, True, True)

        key_bytes = keep.tile([P, H], U8, name="key_bytes")
        nc.vector.tensor_copy(key_bytes[:], d_bytes[:].indirect(kidx_sb[:]))
        key_bytes_dealt = keep.tile([P, H], U8, name="key_bytes_dealt", tag="dealt_w_raw")
        nc.vector.tensor_copy(key_bytes_dealt[:].rearrange("p (t m) -> p m t", t=PACK), key_bytes[:].rearrange("p (m t) -> p m t", t=PACK))
        for odd in range(2):
            for r in range(2):
                nc.sync.dma_start(
                    key_scales[2 * odd + r : P : QUADRANT, :].bitcast(I32),
                    key_bytes_dealt[LIST_ROWS * odd + r : P : QUADRANT, :].bitcast(I32),
                )
        gk_sb = keep.tile([P, PACK], F32, name="gk_sb")
        nc.sync.dma_start(gk_sb[:], gk.rearrange("(p t) o -> p (t o)", t=PACK))
        n3_sb = load_list(n3, "n3_sb")
        n4_sb = load_list(n4, "n4_sb")
        n2_sb = load_list(n2, "n2_sb")
        n5_sb = load_list(n5, "n5_sb")

        w_raw = keep.tile([P, 2 * PACK * N], F32, name="w_raw", tag="dealt_w_raw")
        w3_raw, w2_raw = w_raw[:, : PACK * N], w_raw[:, PACK * N :]
        nc.sync.dma_start(w3_raw, w3.rearrange("(p j) c -> p (j c)", j=PACK))
        nc.sync.dma_start(w2_raw, w2.rearrange("(p j) c -> p (j c)", j=PACK))
        x_two = gather_tokens(two_sb, "x_two", "x_two_words")
        key_words = keep.tile([P, H], U32, name="key_words")
        nc.vector.tensor_copy(key_words[:], d_table[:].indirect(kidx_sb[:]))
        key_codes = keep.tile([P, H], U32, align_bytes=64, name="key_codes", tag="key_codes")
        nc.vector.tensor_copy(key_codes[:].rearrange("p (t m) -> p m t", t=PACK), key_words[:].rearrange("p (m t) -> p m t", t=PACK))
        s_acc = [psum.tile([P, S], F32, name="s_acc%d" % t, tag="bank_b%d" % t) for t in range(PACK)]
        for t in range(PACK):
            product(s_acc[t][:], (key_codes, key_scales), slice(t * P, (t + 1) * P), x_two, True, True)

        gk_zero = keep.tile([P, PACK], F32, name="gk_zero")
        gk_safe = keep.tile([P, PACK], F32, name="gk_safe")
        gk_rec = keep.tile([P, PACK], F32, name="gk_rec")
        nc.gpsimd.tensor_scalar(gk_zero[:], gk_sb[:], 0.0, 1.0, ALU.is_equal, ALU.mult)
        nc.gpsimd.tensor_tensor(gk_safe[:], gk_sb[:], gk_zero[:], ALU.add)
        gk_last = keep.tile([P, 1], F32, name="gk_last")
        nc.gpsimd.tensor_scalar(gk_last[:], gk_sb[:, PACK - 1 :], 0.0625, 1.0, ALU.mult, ALU.mult)
        nc.vector.reciprocal(gk_rec[:], gk_safe[:])

        wide = [keep.tile([P, PACK * S], F32, name="wide%d" % t) for t in range(PACK)]
        y = []
        for t in range(PACK):
            tile = keep.tile([P, S], F32, name="y%d" % t)
            nc.scalar.activation(tile[:], y_acc[t][:], ACT.Copy, scale=gn_abs[:, t : t + 1])
            for first, count in N1_PIECES:
                scalar_gather(wide[t][:, S + first : S + first + count], tile[:].indirect(entries(n1_sb, first, count)))
            y.append(tile)

        num = keep.tile([P, PACK * S], F32, name="num", tag="num_members")
        size = keep.tile([P, PACK * S], F32, name="size", tag="size_recip")
        s = keep.tile([P, PACK * S], F32, name="s", tag="s_mx")
        plane = [slice(t * S, (t + 1) * S) for t in range(PACK)]
        for t in range(PACK - 1):
            nc.vector.tensor_scalar(s[:, plane[t]], s_acc[t][:], gk_sb[:, t : t + 1], 0.0625, ALU.mult, ALU.mult)
        nc.scalar.activation(s[:, plane[-1]], s_acc[-1][:], ACT.Copy, scale=gk_last[:])
        for step in range(PACK + 1):
            if step < PACK:
                for first in (0, HALF):
                    nc.vector.tensor_copy(
                        wide[step][:, 3 * S + first : 3 * S + first + HALF], s[:, plane[step]].indirect(entries(n3_sb, first, HALF))
                    )
            if step >= 1:
                t = step - 1
                nc.vector.tensor_tensor(num[:, plane[t]], s[:, plane[t]], wide[t][:, 3 * S :], ALU.subtract)
                nc.scalar.activation(size[:, plane[t]], num[:, plane[t]], ACT.Abs, scale=gk_rec[:, t : t + 1])
                nc.scalar.activation(wide[t][:, :S], size[:, plane[t]], ACT.Ln, bias=0.5)
        recip = keep.tile([P, PACK * S], F32, name="recip", tag="size_recip")
        for t in range(PACK):
            nc.scalar.activation(recip[:, plane[t]], wide[t][:].indirect(n4_sb[:]), ACT.Exp, scale=-1.0)

        st = keep.tile([P, PACK * S], F32, name="st", tag="st_members")
        mx = keep.tile([P, PACK * S], F32, name="mx", tag="s_mx")
        for t in range(PACK):
            nc.vector.tensor_tensor(mx[:, plane[t]], wide[t][:, S : 3 * S : 2], wide[t][:, S + 1 : 3 * S : 2], ALU.max)
        for t in range(PACK):
            nc.vector.tensor_tensor(st[:, plane[t]], y[t][:], mx[:, plane[t]], ALU.subtract)

        w3_bf = keep.tile([P, PACK * N], BF16, align_bytes=64, name="w3_bf", tag="key_codes")
        nc.vector.tensor_copy(woven(w3_bf[:]), by_lines(w3_raw))
        w2_bf = keep.tile([P, PACK * N], BF16, align_bytes=64, name="w2_bf", tag="x_two_words")
        nc.vector.tensor_tensor(
            woven(w2_bf[:]), by_lines(w2_raw), gn_sign[:].unsqueeze(1).unsqueeze(3).to_broadcast([P, N // PACK, PACK, PACK]), ALU.mult
        )
        w3_q = quantize(w3_bf[:], "w3")
        w2_q = quantize(w2_bf[:], "w2")

        def make_z(first, count, gather):
            st_far = keep.tile([P, PACK * count], F32, name="st_far%d" % first)
            for t in range(PACK):
                gather(st_far[:, t * count : (t + 1) * count], st[:, plane[t]].indirect(entries(n2_sb, first, count)))
            z_bf = keep.tile([P, PACK * count], BF16, align_bytes=64, name="z_bf%d" % first)
            lines = slice(first // PACK, (first + count) // PACK)
            nc.vector.tensor_tensor(woven(z_bf[:]), by_lines(st[:])[:, lines], by_lines(st_far[:]), ALU.max)
            return quantize(z_bf[:], "z%d" % first)

        def make_z2(first, count):
            z2_bf = keep.tile([P, PACK * count], BF16, align_bytes=64, name="z2_bf%d" % first)
            lines = slice(first // PACK, (first + count) // PACK)
            nc.vector.tensor_tensor(woven(z2_bf[:]), by_lines(num[:])[:, lines], by_lines(recip[:])[:, lines], ALU.mult)
            return quantize(z2_bf[:], "z2_%d" % first)

        h = [psum.tile([P, S], F32, name="h_acc%d" % t, tag="bank_a%d" % t) for t in range(OUT_TILES)]

        def add_to_h(weights, codes, first, count, start, stop):
            for t in range(OUT_TILES):
                product(h[t][:, first : first + count], weights, slice(t * P, (t + 1) * P), codes, start, stop)

        add_to_h(w2_q, make_z(*Z_CHUNKS[0], nc.vector.tensor_copy), *Z_CHUNKS[0], True, False)
        for chunk in Z_CHUNKS:
            add_to_h(w3_q, make_z2(*chunk), *chunk, False, False)
        for chunk in Z_CHUNKS[1:]:
            add_to_h(w2_q, make_z(*chunk, scalar_gather), *chunk, False, chunk == Z_CHUNKS[-1])

        h_sb = [keep.tile([P, S], F32, name="h_sb%d" % t) for t in range(TURNED_TILES)]
        nc.vector.tensor_copy(h_sb[1][:], h[1][:])
        for t in range(OUT_TILES):
            nc.scalar.activation(wide[t][:, :S], h[t][:], ACT.Exp)

        units = [(t, 0, S) for t in range(OUT_TILES - 1)] + [(OUT_TILES - 1, first, HALF) for first in (0, HALF)]
        spent = ("size_recip", "s_mx", "num_members", "st_members")
        members = [keep.tile([P, MEMBERS * S], F32, name="members%d" % t, tag=spent[t]) for t in range(OUT_TILES)]
        pairs = {t: keep.tile([P, S, 2], F32, name="pairs%d" % t) for t in range(TURNED_TILES, OUT_TILES)}
        turned = [psum.tile([P, S], F32, name="turned%d" % t, tag="bank_b%d" % t) for t in range(TURNED_TILES)]
        logs = [psum.tile([P, S], F32, name="logs%d" % t, tag="bank_b%d" % (TURNED_TILES + t)) for t in range(TURNED_TILES)]
        work_a = [keep.tile([P, S], F32, name="work_a%d" % t) for t in range(OUT_TILES)]
        work_b = [keep.tile([P, S], F32, name="work_b%d" % t) for t in range(OUT_TILES)]

        def fetch(t, first, count):
            begin, cut, end = MEMBERS * first, MEMBERS * first + VECTOR_ENTRIES[t], MEMBERS * (first + count)
            piece = MEMBERS * P if t == 0 else MEMBERS * S
            for low in range(begin, cut, piece):
                high = min(low + piece, cut)
                nc.vector.tensor_copy(members[t][:, low:high], wide[t][:].indirect(entries(n5_sb, low, high - low)))
            scalar_gather(members[t][:, cut:end], wide[t][:].indirect(entries(n5_sb, cut, end - cut)))

        def add_up(t, first, count):
            halves = (slice(first, first + count // 2), slice(first + count // 2, first + count))
            quads = members[t][:].rearrange("p (j e) -> p j e", e=MEMBERS)
            for cols in halves:
                nc.vector.tensor_tensor(pairs[t][:, cols], quads[:, cols, 0:2], quads[:, cols, 2:4], ALU.add)
            for cols in halves:
                nc.vector.tensor_tensor(work_a[t][:, cols], pairs[t][:, cols, 0], wide[t][:, cols], ALU.add)
            for cols in halves:
                nc.vector.tensor_tensor(work_b[t][:, cols], pairs[t][:, cols, 1], work_a[t][:, cols], ALU.add)

        def finish(t, first, count):
            cols = slice(first, first + count)
            nc.scalar.activation(work_a[t][:, cols], work_b[t][:, cols], ACT.Ln)
            nc.vector.tensor_tensor(work_b[t][:, cols], work_a[t][:, cols], h[t][:, cols], ALU.subtract)
            nc.sync.dma_start(out[t * P : (t + 1) * P, cols], work_b[t][:, cols])

        def add_up_turned(t):
            for b in range(S // P):
                terms = [members[t][:, MEMBERS * P * b + e : MEMBERS * P * (b + 1) : MEMBERS] for e in range(MEMBERS)]
                terms.append(wide[t][:, P * b : P * (b + 1)])
                for e, term in enumerate(terms):
                    nc.tensor.matmul(turned[t][:, P * b : P * (b + 1)], term, identity[:], start=e == 0, stop=e == MEMBERS, is_transpose=True)

        def finish_turned(t):
            nc.scalar.activation(work_a[t][:], turned[t][:], ACT.Ln)
            for b in range(S // P):
                nc.tensor.transpose(logs[t][:, P * b : P * (b + 1)], work_a[t][:, P * b : P * (b + 1)], identity[:])
            nc.vector.tensor_tensor(work_b[t][:], logs[t][:], h_sb[t][:], ALU.subtract)
            nc.sync.dma_start(out[t * P : (t + 1) * P, :], work_b[t][:])

        for unit in units:
            fetch(*unit)
        nc.vector.tensor_copy(h_sb[0][:], h[0][:])
        for t in range(TURNED_TILES):
            add_up_turned(t)
        for unit in units[TURNED_TILES:]:
            add_up(*unit)
        for t in range(TURNED_TILES):
            finish_turned(t)
        for unit in units[TURNED_TILES:]:
            finish(*unit)
